import numpy as np
import ml_dtypes


def mxq(x, axis, fmt="e4m3"):
    dtype, down = {"e4m3": (ml_dtypes.float8_e4m3fn, 7), "e5m2": (ml_dtypes.float8_e5m2, 14)}[fmt]
    v = np.moveaxis(np.asarray(x, np.float32).astype(ml_dtypes.bfloat16).astype(np.float64), axis, -1)
    blocks = v.reshape(v.shape[:-1] + (-1, 32))
    amax = np.abs(blocks).max(-1, keepdims=True)
    byte = np.maximum(np.where(amax > 0, np.frexp(amax)[1] - 1 + 127, 0) - down, 1)
    scale = np.exp2(byte - 127.0)
    codes = (blocks / scale).astype(np.float32).astype(dtype).astype(np.float64)
    return np.moveaxis((codes * scale).reshape(v.shape), -1, axis)


WIDE = False


def mx_kscale(k):
    if not WIDE:
        return np.ones(k)
    levels = np.array([30, -30])
    if k % 512:
        return np.exp2(np.random.permutation(np.resize(levels, k // 32))).repeat(32)
    a = np.empty((k // 512, 16))
    for p in range(k // 512):
        a[p, :8] = np.random.permutation(np.resize(levels, 8))
        for g in range(8):
            far = levels[np.abs(levels - a[p, g]) >= 10]
            a[p, g + 8] = far[np.random.randint(len(far))]
    return np.exp2(a.ravel()).repeat(32)


BF16 = ml_dtypes.bfloat16


def bf(x):
    return np.asarray(x, np.float32).astype(BF16)


def f64(x):
    return np.asarray(x).astype(np.float64)


E2M1 = np.array([0.0, 0.5, 1.0, 1.5, 2.0, 3.0, 4.0, 6.0, -0.0, -0.5, -1.0, -1.5, -2.0, -3.0, -4.0, -6.0])


def pack_weight(w, fmt):
    k, n = w.shape
    w = f64(bf(w)).reshape(k // 32, 32, n)
    amax = np.abs(w).max(1)
    if fmt in ("e4m3", "e5m2"):
        byte = np.frexp(amax)[1] - 1 + 127 - (7 if fmt == "e4m3" else 14)
    else:
        mant, ex = np.frexp(amax / 6.0)
        byte = np.where(mant > 0.5, ex, ex - 1) + 127
    byte = np.clip(np.where(amax > 0, byte, 1), 1, 254)
    scaled = (w * np.exp2(127.0 - byte)[:, None, :]).reshape(k, n).astype(np.float32)
    by_word = np.ascontiguousarray(scaled.reshape(k // 512, 128, 4, n).transpose(0, 1, 3, 2))
    if fmt in ("e4m3", "e5m2"):
        words = by_word.astype(ml_dtypes.float8_e4m3fn if fmt == "e4m3" else ml_dtypes.float8_e5m2).view(np.uint8)
    else:
        c = by_word.astype(ml_dtypes.float4_e2m1fn).view(np.uint8) & 0xF
        words = c[..., 0::2] | (c[..., 1::2] << 4)
    return np.ascontiguousarray(words), np.ascontiguousarray(byte.astype(np.uint8).reshape(k // 512, 16, n))


def unpack_weight(words, scales, fmt):
    g, p, n, _ = words.shape
    if fmt in ("e4m3", "e5m2"):
        vals = np.ascontiguousarray(words).view(ml_dtypes.float8_e4m3fn if fmt == "e4m3" else ml_dtypes.float8_e5m2).astype(np.float64)
    else:
        nib = np.empty((g, p, n, 4), np.uint8)
        nib[..., 0::2] = words & 0xF
        nib[..., 1::2] = words >> 4
        vals = E2M1[nib]
    vals = vals * np.repeat(np.exp2(scales.astype(np.float64) - 127.0), 8, axis=1)[..., None]
    return vals.transpose(0, 1, 3, 2).reshape(g * 512, n)

def planes(Y):
    n, m = Y.shape
    b = f64(bf(Y)).reshape(n // 32, 32, m)
    amax = np.abs(b).max(1)
    byte = np.clip(np.where(amax > 0, np.frexp(amax)[1] - 1 + 127 - 7, 1), 1, 254)
    codes = (b * np.exp2(127.0 - byte)[:, None, :]).reshape(n, m).astype(np.float32).astype(ml_dtypes.float8_e4m3fn).view(np.uint8)
    words = codes.reshape(n // 512, 128, 4, m).transpose(0, 1, 3, 2)
    return np.ascontiguousarray(words), np.ascontiguousarray(byte.astype(np.uint8).reshape(n // 512, 16, m))


MEAS, N, SIG = 1536, 2048, 1024


def setup_inputs():
    s = mx_kscale(N)
    gain = 0.6 * np.exp(0.8 * np.random.randn(MEAS, 1))
    theta = 0.5 + 0.4 * np.random.rand(SIG)
    pseudo = np.random.standard_t(3, size=(N, SIG))
    est = np.sign(pseudo) * np.maximum(np.abs(pseudo) - theta, 0.0)
    onsager = (est != 0).sum(axis=0) / MEAS
    x_words, x_scales = pack_weight(0.6 * est * s[:, None], "e5m2")
    sensing = gain * np.random.randn(MEAS, N) / np.sqrt(MEAS)
    return {
        "x_words": x_words,
        "x_scales": x_scales,
        "sensing": bf(sensing / s[None, :]),
        "measured": bf(gain * np.random.randn(MEAS, SIG)),
        "z_prev": bf(0.8 * gain * np.random.randn(MEAS, SIG)),
        "onsager": bf(onsager),
    }


def reference(x_words, x_scales, sensing, measured, z_prev, onsager):
    X = unpack_weight(x_words, x_scales, "e5m2")
    A = mxq(f64(sensing), 1, "e4m3")
    P = A @ X
    y = f64(measured) - P + f64(onsager) * f64(z_prev)
    Y = y.reshape(MEAS, SIG)
    words, scales = planes(Y)
    return y, words, scales

@@ -1,0 +1,270 @@
+from contextlib import ExitStack
+
+import concourse.mybir as mybir
+from concourse.masks import make_identity
+
+MEAS, COEF, SIG = 1536, 2048, 1024
+FLOPS = 2 * MEAS * COEF * SIG
+
+F32 = mybir.dt.float32
+BF16 = mybir.dt.bfloat16
+I32 = mybir.dt.int32
+U32 = mybir.dt.uint32
+U8 = mybir.dt.uint8
+E4M3X4 = mybir.dt.float8_e4m3fn_x4
+E5M2X4 = mybir.dt.float8_e5m2_x4
+ALU = mybir.AluOpType
+
+P = 128
+PACK = 4
+GROUP = P * PACK
+PASSES = COEF // GROUP
+GROUPS = MEAS // GROUP
+HALF = 512
+HALVES = SIG // HALF
+PAIRS = GROUPS * PACK // 2
+BLOCKS = PAIRS * HALVES
+TRIGGER = 32
+VECTOR_SHARE = 320
+
+
+def tile_amp_onsager_residual_k2_kernel(
+    tc, x_words, x_scales, sensing, measured, z_prev, onsager, out_0, out_1, out_2
+):
+    nc = tc.nc
+
+    def by_slot(dram, g):
+        return dram[GROUP * g : GROUP * (g + 1), :].rearrange("(p t) w -> p t w", t=PACK)
+
+    def place(block):
+        pair, half = divmod(block, HALVES)
+        g, slot_pair = divmod(pair, 2)
+        return g, 2 * slot_pair, half
+
+    with ExitStack() as ctx:
+        keep = ctx.enter_context(tc.tile_pool(name="keep", bufs=1))
+        stage = ctx.enter_context(tc.tile_pool(name="stage", bufs=1))
+        psum = ctx.enter_context(tc.psum_pool(name="psum", bufs=1))
+        ctx.enter_context(tc.manual_schedule())
+
+        identity = keep.tile([P, P], F32, name="identity")
+        make_identity(nc, identity[:])
+        x_plane = keep.tile([P, PASSES, SIG], U8, name="x_plane", align_bytes=64)
+        nc.vector.memset(x_plane[:].bitcast(I32), 0)
+
+        a_rows, z_rows, m_rows, x_codes = {}, {}, {}, {}
+
+        def load_a(tile_no):
+            g, t = divmod(tile_no, PACK)
+            rows = keep.tile([P, COEF], BF16, name="a_rows%d" % tile_no)
+            nc.sync.dma_start(out=rows[:], in_=by_slot(sensing, g)[:, t, :])
+            a_rows[tile_no] = rows
+
+        def load_x(half):
+            codes = keep.tile([P, PASSES, HALF], U32, name="x_codes%d" % half, align_bytes=64)
+            src = x_words.rearrange("c p n t -> p c (n t)")[:, :, PACK * HALF * half : PACK * HALF * (half + 1)]
+            nc.sync.dma_start(out=codes[:].bitcast(I32), in_=src.bitcast(I32))
+            x_codes[half] = codes
+
+        def load_zm(pair):
+            g, slot_pair = divmod(pair, 2)
+            for label, dram, tiles in (("z", z_prev, z_rows), ("m", measured, m_rows)):
+                rows = keep.tile([P, 2, SIG], BF16, name="%s_rows%d" % (label, pair))
+                nc.sync.dma_start(out=rows[:], in_=by_slot(dram, g)[:, 2 * slot_pair : 2 * slot_pair + 2, :])
+                tiles[pair] = rows
+
+        factor_rows = keep.tile([P, SIG // P], BF16, name="factor_rows")
+        nc.sync.dma_start(out=factor_rows[:], in_=onsager.rearrange("(p w) -> p w", p=P))
+        load_a(0)
+        load_a(1)
+        for q in range(4):
+            nc.sync.dma_start(
+                out=x_plane[32 * q : 32 * q + 4, :, :].bitcast(I32),
+                in_=x_scales[:, 4 * q : 4 * q + 4, :].rearrange("c r n -> r c n").bitcast(I32),
+            )
+        load_x(0)
+        load_zm(0)
+        load_a(2)
+        load_a(3)
+        load_x(1)
+        for pair in range(1, PAIRS):
+            load_zm(pair)
+            if pair + 1 < PAIRS:
+                load_a(2 * pair + 2)
+                load_a(2 * pair + 3)
+
+        factor_bank = psum.tile([P, SIG // 2], F32, name="factor_bank")
+        factor_words = factor_rows[:].bitcast(F32)
+        for w in range(4):
+            nc.tensor.transpose(
+                factor_bank[:, w : SIG // 2 : 4], factor_words[:, w : w + 1].to_broadcast([P, P]), identity[:]
+            )
+        factors = factor_bank[:].bitcast(BF16)
+
+        y = {
+            (g, half): keep.tile([P, PACK, HALF], F32, name="y%d_%d" % (g, half))
+            for g in range(GROUPS)
+            for half in range(HALVES)
+        }
+        y_planes = [keep.tile([P, SIG], U8, name="y_plane%d" % g, align_bytes=64) for g in range(GROUPS)]
+        a_turned, a_codes, a_plane, sums, y_bf16 = {}, {}, {}, {}, {}
+
+        def turn_a(tile_no):
+            words = a_rows[tile_no][:].bitcast(F32)
+            turned = stage.tile([P, COEF], BF16, name="a_turned", bufs=3, align_bytes=64)
+            for bank_no in range(2):
+                bank = psum.tile([P, 2, 2, P], F32, name="turn_bank", bufs=3)
+                for c in range(2):
+                    first = 256 * (2 * bank_no + c)
+                    for u in range(2):
+                        nc.tensor.transpose(bank[:, c, u, :], words[:, first + u : first + 256 : 2], identity[:])
+                nc.scalar.copy(
+                    out=turned[:, 1024 * bank_no : 1024 * (bank_no + 1)].bitcast(F32).rearrange("p (c r u) -> p c r u", c=2, u=2),
+                    in_=bank[:].rearrange("p c u r -> p c r u"),
+                )
+            a_turned[tile_no] = turned
+
+        def quantise_a(tile_no):
+            codes = stage.tile([P, PASSES * P], U32, name="a_codes", bufs=5, align_bytes=64)
+            plane = stage.tile([P, PASSES * P], U8, name="a_plane", bufs=5, align_bytes=64)
+            nc.vector.quantize_mx(out=codes[:].bitcast(E4M3X4), scales=plane[:], in_=a_turned[tile_no][:])
+            a_codes[tile_no], a_plane[tile_no] = codes, plane
+
+        def multiply(block):
+            g, slot, half = place(block)
+            for t in (slot, slot + 1):
+                tile_no = PACK * g + t
+                acc = psum.tile([P, HALF], F32, name="acc", bufs=4)
+                for c in range(PASSES):
+                    nc.tensor.matmul_mx(
+                        out=acc[:],
+                        lhsT=a_codes[tile_no][:, P * c : P * (c + 1)].bitcast(E4M3X4),
+                        lhsT_scale=a_plane[tile_no][:, P * c : P * (c + 1)],
+                        rhs=x_codes[half][:, c, :].bitcast(E5M2X4),
+                        rhs_scale=x_plane[:, c, HALF * half : HALF * (half + 1)],
+                        start=(c == 0),
+                        stop=(c == PASSES - 1),
+                    )
+                sums[block, t] = acc
+
+        def scale_z(block, row, lo, hi):
+            g, slot, half = place(block)
+            cols = slice(HALF * half + lo, HALF * half + hi)
+            nc.vector.tensor_tensor(
+                out=y[g, half][:, slot + row, lo:hi],
+                in0=z_rows[block // HALVES][:, row, cols],
+                in1=factors[:, cols],
+                op=ALU.mult,
+            )
+
+        def start_terms(block):
+            scale_z(block, 0, 0, HALF)
+            scale_z(block, 1, 0, HALF - TRIGGER)
+
+        def finish_terms(block):
+            g, slot, half = place(block)
+            scale_z(block, 1, HALF - TRIGGER, HALF)
+            rows = y[g, half][:, slot : slot + 2, :]
+            nc.gpsimd.tensor_tensor(
+                out=rows,
+                in0=rows,
+                in1=m_rows[block // HALVES][:, :, HALF * half : HALF * (half + 1)],
+                op=ALU.add,
+            )
+
+        def store_y(g, half, lo, hi):
+            nc.sync.dma_start(
+                out=by_slot(out_0, g)[:, lo:hi, HALF * half : HALF * (half + 1)], in_=y[g, half][:, lo:hi, :]
+            )
+
+        def subtract(block):
+            g, slot, half = place(block)
+            for t in (slot, slot + 1):
+                row = y[g, half][:, t, :]
+                nc.vector.tensor_tensor(out=row, in0=row, in1=sums[block, t][:], op=ALU.subtract)
+                if block == BLOCKS - 1:
+                    store_y(g, half, t, t + 1)
+            if block < BLOCKS - 1:
+                store_y(g, half, slot, slot + 2)
+
+        def round_y(g, half, copy, lo, hi):
+            if (g, half) not in y_bf16:
+                y_bf16[g, half] = stage.tile([P, HALF, PACK], BF16, name="y_bf16", bufs=2, align_bytes=64)
+            copy(
+                out=y_bf16[g, half][:, lo:hi, :].rearrange("p (c i) t -> p c t i", i=4),
+                in_=y[g, half][:, :, lo:hi].rearrange("p t (c i) -> p c t i", i=4),
+            )
+
+        def quantise_y(g, half):
+            codes = keep.tile([P, HALF], U32, name="y_codes%d_%d" % (g, half), align_bytes=64)
+            nc.vector.quantize_mx(
+                out=codes[:].bitcast(E4M3X4),
+                scales=y_planes[g][:, HALF * half : HALF * (half + 1)],
+                in_=y_bf16[g, half][:].rearrange("p n t -> p (n t)"),
+            )
+            dst = out_1[g].rearrange("p n t -> p (n t)")[:, PACK * HALF * half : PACK * HALF * (half + 1)]
+            nc.sync.dma_start(out=dst.bitcast(I32), in_=codes[:].bitcast(I32))
+            if half == HALVES - 1:
+                queue = nc.scalar if g == GROUPS - 1 else nc.sync
+                for q in range(4):
+                    queue.dma_start(
+                        out=out_2[g, 4 * q : 4 * q + 4, :].bitcast(I32),
+                        in_=y_planes[g][32 * q : 32 * q + 4, :].bitcast(I32),
+                    )
+
+        turn_a(0)
+        turn_a(1)
+        quantise_a(0)
+        quantise_a(1)
+        multiply(0)
+        for block in (0, 1):
+            start_terms(block)
+            finish_terms(block)
+        subtract(0)
+        turn_a(2)
+        turn_a(3)
+        quantise_a(2)
+        quantise_a(3)
+        multiply(1)
+        start_terms(2)
+        finish_terms(2)
+        multiply(2)
+        subtract(1)
+        start_terms(3)
+        finish_terms(3)
+        start_terms(4)
+
+        for block in range(2, BLOCKS - 2, 2):
+            g, slot, half = place(block)
+            turn_a(block + 2)
+            turn_a(block + 3)
+            if slot == 0:
+                round_y(g - 1, 1, nc.scalar.copy, 0, HALF)
+            quantise_a(block + 2)
+            if slot == 0:
+                quantise_y(g - 1, 0)
+            quantise_a(block + 3)
+            multiply(block + 1)
+            finish_terms(block + 2)
+            subtract(block)
+            start_terms(block + 3)
+            if slot == 2:
+                round_y(g, 0, nc.scalar.copy, 0, HALF)
+            multiply(block + 2)
+            if slot == 0 and g < GROUPS - 1:
+                quantise_y(g - 1, 1)
+            finish_terms(block + 3)
+            subtract(block + 1)
+            if block + 4 < BLOCKS:
+                start_terms(block + 4)
+
+        last = GROUPS - 1
+        multiply(BLOCKS - 1)
+        subtract(BLOCKS - 2)
+        round_y(last, 0, nc.scalar.copy, 0, HALF)
+        quantise_y(last - 1, 1)
+        subtract(BLOCKS - 1)
+        round_y(last, 1, nc.vector.tensor_copy, 0, VECTOR_SHARE)
+        round_y(last, 1, nc.scalar.copy, VECTOR_SHARE, HALF)
+        quantise_y(last, 0)
+        quantise_y(last, 1)

@@ -24,8 +24,11 @@ HALF = 512
 HALVES = SIG // HALF
 PAIRS = GROUPS * PACK // 2
 BLOCKS = PAIRS * HALVES
+QUARTER = HALF // 2
 TRIGGER = 32
-VECTOR_SHARE = 320
+VECTOR_ADDS = 192
+VECTOR_ROUNDS = 384
+HEAD_BLOCKS = 3
 
 
 def tile_amp_onsager_residual_k2_kernel(
@@ -66,32 +69,36 @@ def tile_amp_onsager_residual_k2_kernel(
             nc.sync.dma_start(out=codes[:].bitcast(I32), in_=src.bitcast(I32))
             x_codes[half] = codes
 
-        def load_zm(pair):
+        def load_rows(label, dram, tiles, pair):
             g, slot_pair = divmod(pair, 2)
-            for label, dram, tiles in (("z", z_prev, z_rows), ("m", measured, m_rows)):
-                rows = keep.tile([P, 2, SIG], BF16, name="%s_rows%d" % (label, pair))
-                nc.sync.dma_start(out=rows[:], in_=by_slot(dram, g)[:, 2 * slot_pair : 2 * slot_pair + 2, :])
-                tiles[pair] = rows
+            rows = keep.tile([P, 2, SIG], BF16, name="%s_rows%d" % (label, pair))
+            nc.sync.dma_start(out=rows[:], in_=by_slot(dram, g)[:, 2 * slot_pair : 2 * slot_pair + 2, :])
+            tiles[pair] = rows
 
         factor_rows = keep.tile([P, SIG // P], BF16, name="factor_rows")
         nc.sync.dma_start(out=factor_rows[:], in_=onsager.rearrange("(p w) -> p w", p=P))
         load_a(0)
         load_a(1)
+        load_rows("z", z_prev, z_rows, 0)
         for q in range(4):
             nc.sync.dma_start(
                 out=x_plane[32 * q : 32 * q + 4, :, :].bitcast(I32),
                 in_=x_scales[:, 4 * q : 4 * q + 4, :].rearrange("c r n -> r c n").bitcast(I32),
             )
         load_x(0)
-        load_zm(0)
+        load_rows("m", measured, m_rows, 0)
         load_a(2)
+        load_rows("z", z_prev, z_rows, 1)
         load_a(3)
         load_x(1)
-        for pair in range(1, PAIRS):
-            load_zm(pair)
+        load_rows("m", measured, m_rows, 1)
+        load_a(4)
+        for pair in range(2, PAIRS):
+            load_a(2 * pair + 1)
+            load_rows("z", z_prev, z_rows, pair)
             if pair + 1 < PAIRS:
                 load_a(2 * pair + 2)
-                load_a(2 * pair + 3)
+            load_rows("m", measured, m_rows, pair)
 
         factor_bank = psum.tile([P, SIG // 2], F32, name="factor_bank")
         factor_words = factor_rows[:].bitcast(F32)
@@ -106,6 +113,7 @@ def tile_amp_onsager_residual_k2_kernel(
             for g in range(GROUPS)
             for half in range(HALVES)
         }
+        y_codes = {key: keep.tile([P, HALF], U32, name="y_codes%d_%d" % key, align_bytes=64) for key in y}
         y_planes = [keep.tile([P, SIG], U8, name="y_plane%d" % g, align_bytes=64) for g in range(GROUPS)]
         a_turned, a_codes, a_plane, sums, y_bf16 = {}, {}, {}, {}, {}
 
@@ -157,20 +165,27 @@ def tile_amp_onsager_residual_k2_kernel(
                 op=ALU.mult,
             )
 
-        def start_terms(block):
-            scale_z(block, 0, 0, HALF)
-            scale_z(block, 1, 0, HALF - TRIGGER)
-
-        def finish_terms(block):
+        def add_measured(engine, block, lo, hi):
             g, slot, half = place(block)
-            scale_z(block, 1, HALF - TRIGGER, HALF)
-            rows = y[g, half][:, slot : slot + 2, :]
-            nc.gpsimd.tensor_tensor(
+            rows = y[g, half][:, slot : slot + 2, lo:hi]
+            engine.tensor_tensor(
                 out=rows,
                 in0=rows,
-                in1=m_rows[block // HALVES][:, :, HALF * half : HALF * (half + 1)],
+                in1=m_rows[block // HALVES][:, :, HALF * half + lo : HALF * half + hi],
                 op=ALU.add,
             )
+
+        def start_terms(block):
+            scale_z(block, 0, 0, HALF)
+            scale_z(block, 1, 0, HALF if block < HEAD_BLOCKS else HALF - TRIGGER)
+
+        def finish_terms(block):
+            if block < HEAD_BLOCKS:
+                add_measured(nc.vector, block, 0, HALF)
+            else:
+                add_measured(nc.vector, block, 0, VECTOR_ADDS)
+                scale_z(block, 1, HALF - TRIGGER, HALF)
+                add_measured(nc.gpsimd, block, VECTOR_ADDS, HALF)
 
         def store_y(g, half, lo, hi):
             nc.sync.dma_start(
@@ -189,82 +204,73 @@ def tile_amp_onsager_residual_k2_kernel(
 
         def round_y(g, half, copy, lo, hi):
             if (g, half) not in y_bf16:
-                y_bf16[g, half] = stage.tile([P, HALF, PACK], BF16, name="y_bf16", bufs=2, align_bytes=64)
-            copy(
-                out=y_bf16[g, half][:, lo:hi, :].rearrange("p (c i) t -> p c t i", i=4),
-                in_=y[g, half][:, :, lo:hi].rearrange("p t (c i) -> p c t i", i=4),
-            )
+                y_bf16[g, half] = stage.tile([P, HALF, PACK], BF16, name="y_bf16", bufs=3, align_bytes=64)
+            copy(out=y_bf16[g, half][:, lo:hi, :], in_=y[g, half][:, :, lo:hi].rearrange("p t n -> p n t"))
 
-        def quantise_y(g, half):
-            codes = keep.tile([P, HALF], U32, name="y_codes%d_%d" % (g, half), align_bytes=64)
+        def quantise_y(g, half, lo, hi):
+            codes = y_codes[g, half]
             nc.vector.quantize_mx(
-                out=codes[:].bitcast(E4M3X4),
-                scales=y_planes[g][:, HALF * half : HALF * (half + 1)],
-                in_=y_bf16[g, half][:].rearrange("p n t -> p (n t)"),
+                out=codes[:, lo:hi].bitcast(E4M3X4),
+                scales=y_planes[g][:, HALF * half + lo : HALF * half + hi],
+                in_=y_bf16[g, half][:, lo:hi, :].rearrange("p n t -> p (n t)"),
             )
+            if hi < HALF:
+                return
             dst = out_1[g].rearrange("p n t -> p (n t)")[:, PACK * HALF * half : PACK * HALF * (half + 1)]
             nc.sync.dma_start(out=dst.bitcast(I32), in_=codes[:].bitcast(I32))
             if half == HALVES - 1:
-                queue = nc.scalar if g == GROUPS - 1 else nc.sync
                 for q in range(4):
+                    queue = nc.scalar if g == GROUPS - 1 and q >= 2 else nc.sync
                     queue.dma_start(
                         out=out_2[g, 4 * q : 4 * q + 4, :].bitcast(I32),
                         in_=y_planes[g][32 * q : 32 * q + 4, :].bitcast(I32),
                     )
 
+        def quarter(number):
+            g, rest = divmod(number, 4)
+            half, part = divmod(rest, 2)
+            return g, half, QUARTER * part, QUARTER * (part + 1)
+
         turn_a(0)
         turn_a(1)
+        start_terms(0)
+        start_terms(1)
         quantise_a(0)
         quantise_a(1)
         multiply(0)
-        for block in (0, 1):
-            start_terms(block)
-            finish_terms(block)
+        finish_terms(0)
+        finish_terms(1)
         subtract(0)
         turn_a(2)
+        start_terms(2)
         turn_a(3)
         quantise_a(2)
-        quantise_a(3)
         multiply(1)
-        start_terms(2)
-        finish_terms(2)
-        multiply(2)
-        subtract(1)
         start_terms(3)
-        finish_terms(3)
-        start_terms(4)
+        finish_terms(2)
 
-        for block in range(2, BLOCKS - 2, 2):
-            g, slot, half = place(block)
-            turn_a(block + 2)
-            turn_a(block + 3)
-            if slot == 0:
-                round_y(g - 1, 1, nc.scalar.copy, 0, HALF)
+        for block in range(1, BLOCKS - 2):
+            if block + 3 < BLOCKS:
+                turn_a(block + 3)
             quantise_a(block + 2)
-            if slot == 0:
-                quantise_y(g - 1, 0)
-            quantise_a(block + 3)
             multiply(block + 1)
+            if block >= 4:
+                quantise_y(*quarter(block - 4))
             finish_terms(block + 2)
             subtract(block)
-            start_terms(block + 3)
-            if slot == 2:
-                round_y(g, 0, nc.scalar.copy, 0, HALF)
-            multiply(block + 2)
-            if slot == 0 and g < GROUPS - 1:
-                quantise_y(g - 1, 1)
-            finish_terms(block + 3)
-            subtract(block + 1)
-            if block + 4 < BLOCKS:
-                start_terms(block + 4)
+            if block + 3 < BLOCKS:
+                start_terms(block + 3)
+            if block >= 2:
+                g, half, lo, hi = quarter(block - 2)
+                round_y(g, half, nc.scalar.copy, lo, hi)
 
         last = GROUPS - 1
         multiply(BLOCKS - 1)
         subtract(BLOCKS - 2)
         round_y(last, 0, nc.scalar.copy, 0, HALF)
-        quantise_y(last - 1, 1)
+        quantise_y(last - 1, 1, 0, HALF)
         subtract(BLOCKS - 1)
-        round_y(last, 1, nc.vector.tensor_copy, 0, VECTOR_SHARE)
-        round_y(last, 1, nc.scalar.copy, VECTOR_SHARE, HALF)
-        quantise_y(last, 0)
-        quantise_y(last, 1)
+        round_y(last, 1, nc.vector.tensor_copy, 0, VECTOR_ROUNDS)
+        round_y(last, 1, nc.scalar.copy, VECTOR_ROUNDS, HALF)
+        quantise_y(last, 0, 0, HALF)
+        quantise_y(last, 1, 0, HALF)

from contextlib import ExitStack

import concourse.mybir as mybir
from concourse.masks import make_identity

MEAS, COEF, SIG = 1536, 2048, 1024
FLOPS = 2 * MEAS * COEF * SIG

F32 = mybir.dt.float32
BF16 = mybir.dt.bfloat16
I32 = mybir.dt.int32
U32 = mybir.dt.uint32
U8 = mybir.dt.uint8
E4M3X4 = mybir.dt.float8_e4m3fn_x4
E5M2X4 = mybir.dt.float8_e5m2_x4
ALU = mybir.AluOpType

P = 128
PACK = 4
GROUP = P * PACK
PASSES = COEF // GROUP
GROUPS = MEAS // GROUP
HALF = 512
HALVES = SIG // HALF
PAIRS = GROUPS * PACK // 2
BLOCKS = PAIRS * HALVES
QUARTER = HALF // 2
TRIGGER = 32
VECTOR_ADDS = 192
VECTOR_ROUNDS = 384
HEAD_BLOCKS = 3


def tile_amp_onsager_residual_k2_kernel(
    tc, x_words, x_scales, sensing, measured, z_prev, onsager, out_0, out_1, out_2
):
    nc = tc.nc

    def by_slot(dram, g):
        return dram[GROUP * g : GROUP * (g + 1), :].rearrange("(p t) w -> p t w", t=PACK)

    def place(block):
        pair, half = divmod(block, HALVES)
        g, slot_pair = divmod(pair, 2)
        return g, 2 * slot_pair, half

    with ExitStack() as ctx:
        keep = ctx.enter_context(tc.tile_pool(name="keep", bufs=1))
        stage = ctx.enter_context(tc.tile_pool(name="stage", bufs=1))
        psum = ctx.enter_context(tc.psum_pool(name="psum", bufs=1))
        ctx.enter_context(tc.manual_schedule())

        identity = keep.tile([P, P], F32, name="identity")
        make_identity(nc, identity[:])
        x_plane = keep.tile([P, PASSES, SIG], U8, name="x_plane", align_bytes=64)
        nc.vector.memset(x_plane[:].bitcast(I32), 0)

        a_rows, z_rows, m_rows, x_codes = {}, {}, {}, {}

        def load_a(tile_no):
            g, t = divmod(tile_no, PACK)
            rows = keep.tile([P, COEF], BF16, name="a_rows%d" % tile_no)
            nc.sync.dma_start(out=rows[:], in_=by_slot(sensing, g)[:, t, :])
            a_rows[tile_no] = rows

        def load_x(half):
            codes = keep.tile([P, PASSES, HALF], U32, name="x_codes%d" % half, align_bytes=64)
            src = x_words.rearrange("c p n t -> p c (n t)")[:, :, PACK * HALF * half : PACK * HALF * (half + 1)]
            nc.sync.dma_start(out=codes[:].bitcast(I32), in_=src.bitcast(I32))
            x_codes[half] = codes

        def load_rows(label, dram, tiles, pair):
            g, slot_pair = divmod(pair, 2)
            rows = keep.tile([P, 2, SIG], BF16, name="%s_rows%d" % (label, pair))
            nc.sync.dma_start(out=rows[:], in_=by_slot(dram, g)[:, 2 * slot_pair : 2 * slot_pair + 2, :])
            tiles[pair] = rows

        factor_rows = keep.tile([P, SIG // P], BF16, name="factor_rows")
        nc.sync.dma_start(out=factor_rows[:], in_=onsager.rearrange("(p w) -> p w", p=P))
        load_a(0)
        load_a(1)
        load_rows("z", z_prev, z_rows, 0)
        for q in range(4):
            nc.sync.dma_start(
                out=x_plane[32 * q : 32 * q + 4, :, :].bitcast(I32),
                in_=x_scales[:, 4 * q : 4 * q + 4, :].rearrange("c r n -> r c n").bitcast(I32),
            )
        load_x(0)
        load_rows("m", measured, m_rows, 0)
        load_a(2)
        load_rows("z", z_prev, z_rows, 1)
        load_a(3)
        load_x(1)
        load_rows("m", measured, m_rows, 1)
        load_a(4)
        for pair in range(2, PAIRS):
            load_a(2 * pair + 1)
            load_rows("z", z_prev, z_rows, pair)
            if pair + 1 < PAIRS:
                load_a(2 * pair + 2)
            load_rows("m", measured, m_rows, pair)

        factor_bank = psum.tile([P, SIG // 2], F32, name="factor_bank")
        factor_words = factor_rows[:].bitcast(F32)
        for w in range(4):
            nc.tensor.transpose(
                factor_bank[:, w : SIG // 2 : 4], factor_words[:, w : w + 1].to_broadcast([P, P]), identity[:]
            )
        factors = factor_bank[:].bitcast(BF16)

        y = {
            (g, half): keep.tile([P, PACK, HALF], F32, name="y%d_%d" % (g, half))
            for g in range(GROUPS)
            for half in range(HALVES)
        }
        y_codes = {key: keep.tile([P, HALF], U32, name="y_codes%d_%d" % key, align_bytes=64) for key in y}
        y_planes = [keep.tile([P, SIG], U8, name="y_plane%d" % g, align_bytes=64) for g in range(GROUPS)]
        a_turned, a_codes, a_plane, sums, y_bf16 = {}, {}, {}, {}, {}

        def turn_a(tile_no):
            words = a_rows[tile_no][:].bitcast(F32)
            turned = stage.tile([P, COEF], BF16, name="a_turned", bufs=3, align_bytes=64)
            for bank_no in range(2):
                bank = psum.tile([P, 2, 2, P], F32, name="turn_bank", bufs=3)
                for c in range(2):
                    first = 256 * (2 * bank_no + c)
                    for u in range(2):
                        nc.tensor.transpose(bank[:, c, u, :], words[:, first + u : first + 256 : 2], identity[:])
                nc.scalar.copy(
                    out=turned[:, 1024 * bank_no : 1024 * (bank_no + 1)].bitcast(F32).rearrange("p (c r u) -> p c r u", c=2, u=2),
                    in_=bank[:].rearrange("p c u r -> p c r u"),
                )
            a_turned[tile_no] = turned

        def quantise_a(tile_no):
            codes = stage.tile([P, PASSES * P], U32, name="a_codes", bufs=5, align_bytes=64)
            plane = stage.tile([P, PASSES * P], U8, name="a_plane", bufs=5, align_bytes=64)
            nc.vector.quantize_mx(out=codes[:].bitcast(E4M3X4), scales=plane[:], in_=a_turned[tile_no][:])
            a_codes[tile_no], a_plane[tile_no] = codes, plane

        def multiply(block):
            g, slot, half = place(block)
            for t in (slot, slot + 1):
                tile_no = PACK * g + t
                acc = psum.tile([P, HALF], F32, name="acc", bufs=4)
                for c in range(PASSES):
                    nc.tensor.matmul_mx(
                        out=acc[:],
                        lhsT=a_codes[tile_no][:, P * c : P * (c + 1)].bitcast(E4M3X4),
                        lhsT_scale=a_plane[tile_no][:, P * c : P * (c + 1)],
                        rhs=x_codes[half][:, c, :].bitcast(E5M2X4),
                        rhs_scale=x_plane[:, c, HALF * half : HALF * (half + 1)],
                        start=(c == 0),
                        stop=(c == PASSES - 1),
                    )
                sums[block, t] = acc

        def scale_z(block, row, lo, hi):
            g, slot, half = place(block)
            cols = slice(HALF * half + lo, HALF * half + hi)
            nc.vector.tensor_tensor(
                out=y[g, half][:, slot + row, lo:hi],
                in0=z_rows[block // HALVES][:, row, cols],
                in1=factors[:, cols],
                op=ALU.mult,
            )

        def add_measured(engine, block, lo, hi):
            g, slot, half = place(block)
            rows = y[g, half][:, slot : slot + 2, lo:hi]
            engine.tensor_tensor(
                out=rows,
                in0=rows,
                in1=m_rows[block // HALVES][:, :, HALF * half + lo : HALF * half + hi],
                op=ALU.add,
            )

        def start_terms(block):
            scale_z(block, 0, 0, HALF)
            scale_z(block, 1, 0, HALF if block < HEAD_BLOCKS else HALF - TRIGGER)

        def finish_terms(block):
            if block < HEAD_BLOCKS:
                add_measured(nc.vector, block, 0, HALF)
            else:
                add_measured(nc.vector, block, 0, VECTOR_ADDS)
                scale_z(block, 1, HALF - TRIGGER, HALF)
                add_measured(nc.gpsimd, block, VECTOR_ADDS, HALF)

        def store_y(g, half, lo, hi):
            nc.sync.dma_start(
                out=by_slot(out_0, g)[:, lo:hi, HALF * half : HALF * (half + 1)], in_=y[g, half][:, lo:hi, :]
            )

        def subtract(block):
            g, slot, half = place(block)
            for t in (slot, slot + 1):
                row = y[g, half][:, t, :]
                nc.vector.tensor_tensor(out=row, in0=row, in1=sums[block, t][:], op=ALU.subtract)
                if block == BLOCKS - 1:
                    store_y(g, half, t, t + 1)
            if block < BLOCKS - 1:
                store_y(g, half, slot, slot + 2)

        def round_y(g, half, copy, lo, hi):
            if (g, half) not in y_bf16:
                y_bf16[g, half] = stage.tile([P, HALF, PACK], BF16, name="y_bf16", bufs=3, align_bytes=64)
            copy(out=y_bf16[g, half][:, lo:hi, :], in_=y[g, half][:, :, lo:hi].rearrange("p t n -> p n t"))

        def quantise_y(g, half, lo, hi):
            codes = y_codes[g, half]
            nc.vector.quantize_mx(
                out=codes[:, lo:hi].bitcast(E4M3X4),
                scales=y_planes[g][:, HALF * half + lo : HALF * half + hi],
                in_=y_bf16[g, half][:, lo:hi, :].rearrange("p n t -> p (n t)"),
            )
            if hi < HALF:
                return
            dst = out_1[g].rearrange("p n t -> p (n t)")[:, PACK * HALF * half : PACK * HALF * (half + 1)]
            nc.sync.dma_start(out=dst.bitcast(I32), in_=codes[:].bitcast(I32))
            if half == HALVES - 1:
                for q in range(4):
                    queue = nc.scalar if g == GROUPS - 1 and q >= 2 else nc.sync
                    queue.dma_start(
                        out=out_2[g, 4 * q : 4 * q + 4, :].bitcast(I32),
                        in_=y_planes[g][32 * q : 32 * q + 4, :].bitcast(I32),
                    )

        def quarter(number):
            g, rest = divmod(number, 4)
            half, part = divmod(rest, 2)
            return g, half, QUARTER * part, QUARTER * (part + 1)

        turn_a(0)
        turn_a(1)
        start_terms(0)
        start_terms(1)
        quantise_a(0)
        quantise_a(1)
        multiply(0)
        finish_terms(0)
        finish_terms(1)
        subtract(0)
        turn_a(2)
        start_terms(2)
        turn_a(3)
        quantise_a(2)
        multiply(1)
        start_terms(3)
        finish_terms(2)

        for block in range(1, BLOCKS - 2):
            if block + 3 < BLOCKS:
                turn_a(block + 3)
            quantise_a(block + 2)
            multiply(block + 1)
            if block >= 4:
                quantise_y(*quarter(block - 4))
            finish_terms(block + 2)
            subtract(block)
            if block + 3 < BLOCKS:
                start_terms(block + 3)
            if block >= 2:
                g, half, lo, hi = quarter(block - 2)
                round_y(g, half, nc.scalar.copy, lo, hi)

        last = GROUPS - 1
        multiply(BLOCKS - 1)
        subtract(BLOCKS - 2)
        round_y(last, 0, nc.scalar.copy, 0, HALF)
        quantise_y(last - 1, 1, 0, HALF)
        subtract(BLOCKS - 1)
        round_y(last, 1, nc.vector.tensor_copy, 0, VECTOR_ROUNDS)
        round_y(last, 1, nc.scalar.copy, VECTOR_ROUNDS, HALF)
        quantise_y(last, 0, 0, HALF)
        quantise_y(last, 1, 0, HALF)
